import numpy as np
import ml_dtypes


def mxq(x, axis, fmt="e4m3"):
    dtype, down = {"e4m3": (ml_dtypes.float8_e4m3fn, 7), "e5m2": (ml_dtypes.float8_e5m2, 14)}[fmt]
    v = np.moveaxis(np.asarray(x, np.float32).astype(ml_dtypes.bfloat16).astype(np.float64), axis, -1)
    blocks = v.reshape(v.shape[:-1] + (-1, 32))
    amax = np.abs(blocks).max(-1, keepdims=True)
    byte = np.maximum(np.where(amax > 0, np.frexp(amax)[1] - 1 + 127, 0) - down, 1)
    scale = np.exp2(byte - 127.0)
    codes = (blocks / scale).astype(np.float32).astype(dtype).astype(np.float64)
    return np.moveaxis((codes * scale).reshape(v.shape), -1, axis)


WIDE = False


def mx_kscale(k):
    if not WIDE:
        return np.ones(k)
    levels = np.array([10, -10, 5, -5, 0])
    if k % 512:
        return np.exp2(np.random.permutation(np.resize(levels, k // 32))).repeat(32)
    a = np.empty((k // 512, 16))
    for p in range(k // 512):
        a[p, :8] = np.random.permutation(np.resize(levels, 8))
        for g in range(8):
            far = levels[np.abs(levels - a[p, g]) >= 10]
            a[p, g + 8] = far[np.random.randint(len(far))]
    return np.exp2(a.ravel()).repeat(32)


def f64(x):
    return np.asarray(x).astype(np.float64)


def striped(idx):
    return np.tile(idx.reshape(-1, 16).T, (8, 1)).astype(np.uint16)


def unstriped(offs):
    return offs[:16].T.reshape(-1).astype(np.int64)


E2M1 = np.array([0.0, 0.5, 1.0, 1.5, 2.0, 3.0, 4.0, 6.0, -0.0, -0.5, -1.0, -1.5, -2.0, -3.0, -4.0, -6.0])


def pack_weight(w, fmt):
    k, n = w.shape
    w = f64(np.asarray(w, np.float32).astype(ml_dtypes.bfloat16)).reshape(k // 32, 32, n)
    amax = np.abs(w).max(1)
    if fmt == "e4m3":
        byte = np.frexp(amax)[1] - 1 + 127 - 7
    else:
        mant, ex = np.frexp(amax / 6.0)
        byte = np.where(mant > 0.5, ex, ex - 1) + 127
    byte = np.clip(np.where(amax > 0, byte, 1), 1, 254)
    scaled = (w * np.exp2(127.0 - byte)[:, None, :]).reshape(k, n).astype(np.float32)
    by_word = np.ascontiguousarray(scaled.reshape(k // 512, 128, 4, n).transpose(0, 1, 3, 2))
    if fmt == "e4m3":
        words = by_word.astype(ml_dtypes.float8_e4m3fn).view(np.uint8)
    else:
        c = by_word.astype(ml_dtypes.float4_e2m1fn).view(np.uint8) & 0xF
        words = (c[..., 0::2] | (c[..., 1::2] << 4)).reshape(k // 512, 128, 2 * n)
    return np.ascontiguousarray(words), np.ascontiguousarray(byte.astype(np.uint8).reshape(k // 512, 16, n))


def unpack_weight(words, scales, fmt):
    g, _, n = scales.shape
    words = np.ascontiguousarray(words).reshape(g, 128, n, -1)
    if fmt == "e4m3":
        vals = words.view(ml_dtypes.float8_e4m3fn).astype(np.float64)
    else:
        nib = np.empty((g, 128, n, 4), np.uint8)
        nib[..., 0::2] = words & 0xF
        nib[..., 1::2] = words >> 4
        vals = E2M1[nib]
    vals = vals * np.repeat(np.exp2(scales.astype(np.float64) - 127.0), 8, axis=1)[..., None]
    return vals.transpose(0, 1, 3, 2).reshape(g * 512, n)


def gelu(v):
    return 0.5 * v * (1.0 + np.tanh(np.sqrt(2.0 / np.pi) * (v + 0.044715 * v**3)))


K, H, T, S, T2, P = 1536, 512, 2048, 1024, 2048, 512

def setup_inputs():
    n = np.random.standard_normal
    s = mx_kscale(K)[:, None]
    u = mx_kscale(H)[:, None]
    tab_words, tab_scales = pack_weight(n((K, T)) * s, "e4m3")
    w4_words, w4_scales = pack_weight(1.2 * n((K, H)) / np.sqrt(K) / s, "e2m1")
    wd = (0.9 * n((K, H)) / np.sqrt(K) / s).astype(np.float32)
    gain = (1.2 * np.exp(0.3 * n(H)) * u[:, 0]).astype(np.float32)
    res = (0.5 * n((H, S)) * u).astype(np.float32)
    page0 = (n((H, T2)) * u).astype(np.float32)
    wgs = np.exp(0.3 * n((128, S))).astype(np.float32)
    band = (n(H) / u[:, 0] ** 2 / np.sqrt(H)).astype(np.float32)
    bub = np.exp(0.4 * n(P)).astype(np.float32)
    offs = striped(np.random.permutation(T)[:S])
    offs2 = striped(np.random.permutation(T2)[:S])
    offs3 = striped(np.random.permutation(T2)[:P])
    offs4 = striped(np.random.permutation(T2)[:P])
    return dict(tab_words=tab_words, tab_scales=tab_scales, w4_words=w4_words, w4_scales=w4_scales,
                wd=wd, gain=gain, res=res, page0=page0, wgs=wgs, band=band, bub=bub,
                offs=offs, offs2=offs2, offs3=offs3, offs4=offs4)

def reference(tab_words, tab_scales, w4_words, w4_scales, wd, gain, res, page0, wgs, band, bub,
              offs, offs2, offs3, offs4):
    v = unpack_weight(tab_words, tab_scales, "e4m3")[:, unstriped(offs)]
    w4 = unpack_weight(w4_words, w4_scales, "e2m1")
    wdq = mxq(f64(wd), 0, "e4m3")
    f = w4.T @ v + wdq.T @ v
    h = f64(gain)[:, None] * np.tanh(f) + f64(res)
    page = f64(page0).copy()
    page[:, unstriped(offs2)] = np.tile(f64(wgs), (H // 128, 1)) * h
    x1 = page[:, unstriped(offs3)]
    x2 = np.abs(page[:, unstriped(offs4)]) * f64(band)[:, None]
    e = mxq(x1, 0, "e4m3").T @ mxq(x2, 0, "e4m3")
    return f64(bub)[:, None] * e

@@ -1,0 +1,268 @@
+from contextlib import ExitStack
+
+import concourse.mybir as mybir
+
+K, H, T, S, T2, PICKS = 1536, 512, 2048, 1024, 2048, 512
+FLOPS = 2 * (2 * K * H * S) + 2 * H * PICKS * PICKS
+
+F32 = mybir.dt.float32
+BF16 = mybir.dt.bfloat16
+I32 = mybir.dt.int32
+U32 = mybir.dt.uint32
+U16 = mybir.dt.uint16
+U8 = mybir.dt.uint8
+FP8X4 = mybir.dt.float8_e4m3fn_x4
+FP4X4 = mybir.dt.float4_e2m1fn_x4
+MULT = mybir.AluOpType.mult
+ADD = mybir.AluOpType.add
+ACT = mybir.ActivationFunctionType
+
+P = 128
+PACK = 4
+PASSES = K // (P * PACK)
+BANK = 512
+QUAD = 32
+SPARE = {1: 8, 2: 72}
+
+
+def tile_list_bubble_band_match_kernel(
+    tc, tab_words, tab_scales, w4_words, w4_scales, wd, gain, res, page0, wgs, band, bub,
+    offs, offs2, offs3, offs4, out,
+):
+    nc = tc.nc
+    with ExitStack() as ctx:
+        keep = ctx.enter_context(tc.tile_pool(name="keep", bufs=1))
+        psum = ctx.enter_context(tc.psum_pool(name="psum", bufs=1))
+
+        def tile(name, shape, dtype):
+            return keep.tile(shape, dtype, name=name, align_bytes=64)
+
+        def tiles(name, count, shape, dtype):
+            return [tile(f"{name}{i}", shape, dtype) for i in range(count)]
+
+        idx = tile("idx", [P, S // 16], U16)
+        idx2 = tile("idx2", [P, S // 16], U16)
+        idx3 = tile("idx3", [P, PICKS // 16], U16)
+        idx4 = tile("idx4", [P, PICKS // 16], U16)
+        tab = tiles("tab", PASSES, [P, T], I32)
+        tab_sc = tile("tab_sc", [P, T], U8)
+        v_words = tiles("v_words", PASSES, [P, S], U32)
+        v_sc = tiles("v_sc", PASSES, [P, S], U8)
+        w4_raw = tile("w4_raw", [P, PASSES * 2 * H], U8)
+        w4_sc_raw = tile("w4_sc_raw", [P, PASSES * H], U8)
+        w4 = tile("w4", [P, PASSES * 2 * H], U8)
+        w4_sc = tile("w4_sc", [P, PASSES * H], U8)
+        wd_raw = tiles("wd_raw", PASSES, [P, PACK, H], F32)
+        wd_bf = tiles("wd_bf", PASSES, [P, PACK * H], BF16)
+        wd_q = tiles("wd_q", PASSES, [P, H], U32)
+        wd_sc = tiles("wd_sc", PASSES, [P, H], U8)
+        gain_sb = tile("gain_sb", [P, PACK], F32)
+        band_sb = tile("band_sb", [P, PACK], F32)
+        bub_sb = tile("bub_sb", [P, PICKS // P], F32)
+        page = tiles("page", PACK, [P, T2], F32)
+        res_sb = tiles("res_sb", PACK, [P, S], F32)
+        wgs_sb = tiles("wgs_sb", PACK, [P, S], F32)
+        h = tiles("h", PACK, [P, S], F32)
+        picked = tiles("picked", 2, [P, PICKS], F32)
+        size = tile("size", [P, PICKS], F32)
+        x1_bf = tile("x1_bf", [P, PICKS, PACK], BF16)
+        x2_bf = tile("x2_bf", [P, PICKS, PACK], BF16)
+        x1_q = tile("x1_q", [P, PICKS], U32)
+        x2_q = tile("x2_q", [P, PICKS], U32)
+        x1_sc = tile("x1_sc", [P, PICKS], U8)
+        x2_sc = tile("x2_sc", [P, PICKS], U8)
+        out_sb = tiles("out_sb", PICKS // P, [P, PICKS], F32)
+
+        nc.vector.memset(tab_sc[:].bitcast(I32), 0)
+        nc.vector.memset(w4_sc_raw[:].bitcast(I32), 0)
+        for a in range(1, PASSES):
+            nc.vector.memset(v_sc[a][:].bitcast(I32), 0)
+
+        def load_scales(dst, src):
+            for q in range(P // QUAD):
+                nc.sync.dma_start(
+                    out=dst[QUAD * q : QUAD * q + 4, :].bitcast(I32).rearrange("r (a n) -> r a n", a=PASSES),
+                    in_=src.bitcast(I32)[:, 4 * q : 4 * q + 4, :].rearrange("a r n -> r a n"),
+                )
+
+        def load_wd(a):
+            rows = wd[a * P * PACK : (a + 1) * P * PACK, :]
+            nc.sync.dma_start(out=wd_raw[a][:], in_=rows.rearrange("(p j) c -> p j c", j=PACK))
+
+        def load_tab(a):
+            nc.sync.dma_start(out=tab[a][:], in_=tab_words[a].rearrange("p n i -> p (n i)").bitcast(I32))
+
+        res_rows = res.rearrange("(p t) n -> t p n", t=PACK)
+        page_rows = page0.rearrange("(p t) n -> t p n", t=PACK)
+        wgs_rows = wgs.rearrange("(e t) n -> t e n", t=PACK)
+
+        def load_factors(t, lo, hi):
+            nc.sync.dma_start(out=res_sb[t][:, lo:hi], in_=res_rows[t][:, lo:hi])
+            for q in range(P // QUAD):
+                nc.sync.dma_start(out=wgs_sb[t][QUAD * q : QUAD * (q + 1), lo:hi], in_=wgs_rows[t][:, lo:hi])
+
+        def load_page(t):
+            nc.sync.dma_start(out=page[t][:], in_=page_rows[t])
+
+        def load_tab_scales():
+            rows = tab_scales.bitcast(I32)
+            for q in range(P // QUAD):
+                nc.sync.dma_start(
+                    out=tab_sc[QUAD * q : QUAD * q + 4, :].bitcast(I32), in_=rows[0, 4 * q : 4 * q + 4, :]
+                )
+            for a in range(1, PASSES):
+                nc.sync.dma_start(out=tab_sc[SPARE[a] : SPARE[a] + 16, :].bitcast(I32), in_=rows[a])
+
+        nc.sync.dma_start(idx[:], offs)
+        nc.sync.dma_start(idx2[:], offs2)
+        nc.sync.dma_start(idx4[:], offs4)
+        nc.sync.dma_start(idx3[:], offs3)
+        nc.sync.dma_start(out=gain_sb[:], in_=gain.rearrange("(p t) -> p t", t=PACK))
+        nc.sync.dma_start(out=band_sb[:], in_=band.rearrange("(p t) -> p t", t=PACK))
+        with nc.allow_non_contiguous_dma(reason="one factor for each partition"):
+            nc.sync.dma_start(out=bub_sb[:], in_=bub.rearrange("(c p) -> p c", p=P))
+        load_tab(0)
+        load_tab_scales()
+        load_wd(0)
+        nc.sync.dma_start(
+            out=w4_raw[:].bitcast(I32).rearrange("p (a n) -> p a n", a=PASSES),
+            in_=w4_words.bitcast(I32).rearrange("a p n -> p a n"),
+        )
+        load_scales(w4_sc_raw, w4_scales)
+        load_wd(1)
+        load_wd(2)
+        load_tab(1)
+        load_tab(2)
+        load_factors(0, 0, BANK)
+        load_page(0)
+        load_factors(0, BANK, S)
+        for t in range(1, PACK):
+            load_factors(t, 0, S)
+            load_page(t)
+
+        def gather_scales():
+            nc.vector.tensor_copy(v_sc[0][:], tab_sc[:].indirect(idx[:]))
+            for a in range(1, PASSES):
+                for q in range(P // QUAD):
+                    row = SPARE[a] + 4 * q
+                    nc.gpsimd.dma_start(
+                        out=v_sc[a][QUAD * q : QUAD * q + 4, :].bitcast(I32),
+                        in_=v_sc[0][row : row + 4, :].bitcast(I32),
+                    )
+
+        def gather_words(a, lo, hi):
+            nc.vector.tensor_copy(
+                v_words[a][:, lo:hi], tab[a][:].bitcast(U32).indirect(idx[:, lo // 16 : hi // 16])
+            )
+
+        def round_wd(a):
+            nc.scalar.copy(
+                out=wd_bf[a][:].rearrange("p (t m j) -> p m t j", t=PACK, j=PACK),
+                in_=wd_raw[a][:].rearrange("p j (m t) -> p m t j", t=PACK),
+            )
+
+        def quantize_wd(a):
+            nc.vector.quantize_mx(out=wd_q[a][:].bitcast(FP8X4), scales=wd_sc[a][:], in_=wd_bf[a][:])
+
+        for a in range(PASSES):
+            round_wd(a)
+        gather_scales()
+        gather_words(0, 0, S)
+        nc.vector.tensor_copy(
+            out=w4[:].bitcast(U16).rearrange("p (a t m) -> p a t m", a=PASSES, t=PACK),
+            in_=w4_raw[:].bitcast(U16).rearrange("p (a m t) -> p a t m", a=PASSES, t=PACK),
+        )
+        nc.vector.tensor_copy(
+            out=w4_sc[:].rearrange("p (a t m) -> p a t m", a=PASSES, t=PACK),
+            in_=w4_sc_raw[:].rearrange("p (a m t) -> p a t m", a=PASSES, t=PACK),
+        )
+        quantize_wd(0)
+        quantize_wd(1)
+        quantize_wd(2)
+        gather_words(1, 0, S)
+        gather_words(2, 0, BANK)
+        gather_words(2, BANK, S)
+
+        for t in range(PACK):
+            for lo in range(0, S, BANK):
+                cols = slice(lo, lo + BANK)
+                acc = psum.tile([P, BANK], F32, name="acc", bufs=2)
+                for a in range(PASSES):
+                    c0 = a * H + t * P
+                    moving = v_words[a][:, cols].bitcast(FP8X4)
+                    nc.tensor.matmul_mx(
+                        out=acc[:],
+                        lhsT=wd_q[a][:, t * P : (t + 1) * P].bitcast(FP8X4),
+                        lhsT_scale=wd_sc[a][:, t * P : (t + 1) * P],
+                        rhs=moving, rhs_scale=v_sc[a][:, cols],
+                        start=(a == 0), stop=False,
+                    )
+                    nc.tensor.matmul_mx(
+                        out=acc[:],
+                        lhsT=w4[:, 2 * c0 : 2 * (c0 + P)].bitcast(FP4X4),
+                        lhsT_scale=w4_sc[:, c0 : c0 + P],
+                        rhs=moving, rhs_scale=v_sc[a][:, cols],
+                        start=False, stop=(a == PASSES - 1),
+                    )
+                nc.scalar.activation(out=h[t][:, cols], in_=acc[:], func=ACT.Tanh)
+
+        def finish_h(t, lo, hi):
+            nc.vector.scalar_tensor_tensor(
+                out=h[t][:, lo:hi], in0=h[t][:, lo:hi], scalar=gain_sb[:, t : t + 1],
+                in1=res_sb[t][:, lo:hi], op0=MULT, op1=ADD,
+            )
+
+        def pick_bands(t, lo, hi):
+            dst = picked[t % 2]
+            nc.vector.tensor_copy(dst[:, lo:hi], page[t][:].indirect(idx4[:, lo // 16 : hi // 16]))
+            nc.scalar.activation(out=size[:, lo:hi], in_=dst[:, lo:hi], func=ACT.Abs)
+            nc.scalar.activation(
+                out=x2_bf[:, lo:hi, t], in_=size[:, lo:hi], func=ACT.Copy, scale=band_sb[:, t : t + 1]
+            )
+
+        def put(t, lo, hi):
+            nc.vector.tensor_tensor(
+                page[t][:].indirect(idx2[:, lo // 16 : hi // 16]), h[t][:, lo:hi], wgs_sb[t][:, lo:hi], MULT
+            )
+
+        finish_h(0, 0, BANK)
+        put(0, 0, BANK)
+        finish_h(0, BANK, S)
+        for t in range(PACK):
+            put(t, BANK if t == 0 else 0, S)
+            if t + 1 < PACK:
+                finish_h(t + 1, 0, S)
+                pick_bands(t, 0, PICKS)
+                dst = picked[(t + 1) % 2]
+                nc.vector.tensor_copy(dst[:], page[t][:].indirect(idx3[:]))
+                nc.scalar.copy(out=x1_bf[:, :, t], in_=dst[:])
+            else:
+                pick_bands(t, 0, PICKS // 2)
+                pick_bands(t, PICKS // 2, PICKS)
+                nc.vector.tensor_copy(x1_bf[:, :, t], page[t][:].indirect(idx3[:]))
+
+        def quantize(codes, scales, values, lo, hi):
+            nc.vector.quantize_mx(
+                out=codes[:, lo:hi].bitcast(FP8X4), scales=scales[:, lo:hi],
+                in_=values[:, lo:hi, :].rearrange("p n t -> p (n t)"),
+            )
+
+        half = PICKS // 2
+        quantize(x2_q, x2_sc, x2_bf, 0, half)
+        quantize(x1_q, x1_sc, x1_bf, 0, PICKS)
+        quantize(x2_q, x2_sc, x2_bf, half, PICKS)
+
+        for c in range(PICKS // P):
+            rows = slice(c * P, (c + 1) * P)
+            acc = psum.tile([P, BANK], F32, name="score", bufs=4)
+            nc.tensor.matmul_mx(
+                out=acc[:], lhsT=x1_q[:, rows].bitcast(FP8X4), lhsT_scale=x1_sc[:, rows],
+                rhs=x2_q[:].bitcast(FP8X4), rhs_scale=x2_sc[:], start=True, stop=True,
+            )
+            if c % 2 == 0:
+                nc.scalar.activation(out=out_sb[c][:], in_=acc[:], func=ACT.Copy, scale=bub_sb[:, c : c + 1])
+            else:
+                nc.vector.tensor_scalar(
+                    out=out_sb[c][:], in0=acc[:], scalar1=bub_sb[:, c : c + 1], scalar2=None, op0=MULT
+                )
+            nc.sync.dma_start(out=out[rows, :], in_=out_sb[c][:])

@@ -62,7 +62,8 @@ def tile_list_bubble_band_match_kernel(
         page = tiles("page", PACK, [P, T2], F32)
         res_sb = tiles("res_sb", PACK, [P, S], F32)
         wgs_sb = tiles("wgs_sb", PACK, [P, S], F32)
-        h = tiles("h", PACK, [P, S], F32)
+        bent = tiles("bent", PACK, [P, S], F32)
+        h = tile("h", [P, S], F32)
         picked = tiles("picked", 2, [P, PICKS], F32)
         size = tile("size", [P, PICKS], F32)
         x1_bf = tile("x1_bf", [P, PICKS, PACK], BF16)
@@ -204,11 +205,15 @@ def tile_list_bubble_band_match_kernel(
                         rhs=moving, rhs_scale=v_sc[a][:, cols],
                         start=False, stop=(a == PASSES - 1),
                     )
-                nc.scalar.activation(out=h[t][:, cols], in_=acc[:], func=ACT.Tanh)
+                nc.scalar.activation(out=bent[t][:, cols], in_=acc[:], func=ACT.Tanh)
+                if t > 0:
+                    nc.scalar.activation(
+                        out=bent[t][:, cols], in_=bent[t][:, cols], func=ACT.Copy, scale=gain_sb[:, t : t + 1]
+                    )
 
         def finish_h(t, lo, hi):
             nc.vector.scalar_tensor_tensor(
-                out=h[t][:, lo:hi], in0=h[t][:, lo:hi], scalar=gain_sb[:, t : t + 1],
+                out=h[:, lo:hi], in0=bent[t][:, lo:hi], scalar=gain_sb[:, t : t + 1],
                 in1=res_sb[t][:, lo:hi], op0=MULT, op1=ADD,
             )
 
@@ -222,7 +227,7 @@ def tile_list_bubble_band_match_kernel(
 
         def put(t, lo, hi):
             nc.vector.tensor_tensor(
-                page[t][:].indirect(idx2[:, lo // 16 : hi // 16]), h[t][:, lo:hi], wgs_sb[t][:, lo:hi], MULT
+                page[t][:].indirect(idx2[:, lo // 16 : hi // 16]), h[:, lo:hi], wgs_sb[t][:, lo:hi], MULT
             )
 
         finish_h(0, 0, BANK)
@@ -231,7 +236,7 @@ def tile_list_bubble_band_match_kernel(
         for t in range(PACK):
             put(t, BANK if t == 0 else 0, S)
             if t + 1 < PACK:
-                finish_h(t + 1, 0, S)
+                nc.gpsimd.tensor_tensor(h[:], bent[t + 1][:], res_sb[t + 1][:], ADD)
                 pick_bands(t, 0, PICKS)
                 dst = picked[(t + 1) % 2]
                 nc.vector.tensor_copy(dst[:], page[t][:].indirect(idx3[:]))

@@ -22,7 +22,8 @@ PACK = 4
 PASSES = K // (P * PACK)
 BANK = 512
 QUAD = 32
-SPARE = {1: 8, 2: 72}
+SCALE_ROWS = 16
+FIRST_ROW = P - PASSES * SCALE_ROWS
 
 
 def tile_list_bubble_band_match_kernel(
@@ -47,7 +48,8 @@ def tile_list_bubble_band_match_kernel(
         tab = tiles("tab", PASSES, [P, T], I32)
         tab_sc = tile("tab_sc", [P, T], U8)
         v_words = tiles("v_words", PASSES, [P, S], U32)
-        v_sc = tiles("v_sc", PASSES, [P, S], U8)
+        v_rows = tile("v_rows", [P, S], U8)
+        v_sc = tile("v_sc", [P, PASSES * S], U8)
         w4_raw = tile("w4_raw", [P, PASSES * 2 * H], U8)
         w4_sc_raw = tile("w4_sc_raw", [P, PASSES * H], U8)
         w4 = tile("w4", [P, PASSES * 2 * H], U8)
@@ -74,10 +76,9 @@ def tile_list_bubble_band_match_kernel(
         x2_sc = tile("x2_sc", [P, PICKS], U8)
         out_sb = tiles("out_sb", PICKS // P, [P, PICKS], F32)
 
-        nc.vector.memset(tab_sc[:].bitcast(I32), 0)
         nc.vector.memset(w4_sc_raw[:].bitcast(I32), 0)
-        for a in range(1, PASSES):
-            nc.vector.memset(v_sc[a][:].bitcast(I32), 0)
+        nc.vector.memset(tab_sc[0:FIRST_ROW, :].bitcast(I32), 0)
+        nc.vector.memset(v_sc[:].bitcast(I32), 0)
 
         def load_scales(dst, src):
             for q in range(P // QUAD):
@@ -106,49 +107,45 @@ def tile_list_bubble_band_match_kernel(
             nc.sync.dma_start(out=page[t][:], in_=page_rows[t])
 
         def load_tab_scales():
-            rows = tab_scales.bitcast(I32)
-            for q in range(P // QUAD):
-                nc.sync.dma_start(
-                    out=tab_sc[QUAD * q : QUAD * q + 4, :].bitcast(I32), in_=rows[0, 4 * q : 4 * q + 4, :]
-                )
-            for a in range(1, PASSES):
-                nc.sync.dma_start(out=tab_sc[SPARE[a] : SPARE[a] + 16, :].bitcast(I32), in_=rows[a])
+            rows = tab_scales.bitcast(I32).rearrange("a q n -> (a q) n")
+            for lo, hi in ((0, SCALE_ROWS), (SCALE_ROWS, PASSES * SCALE_ROWS)):
+                nc.sync.dma_start(out=tab_sc[FIRST_ROW + lo : FIRST_ROW + hi, :].bitcast(I32), in_=rows[lo:hi, :])
 
         nc.sync.dma_start(idx[:], offs)
-        nc.sync.dma_start(idx2[:], offs2)
-        nc.sync.dma_start(idx4[:], offs4)
-        nc.sync.dma_start(idx3[:], offs3)
-        nc.sync.dma_start(out=gain_sb[:], in_=gain.rearrange("(p t) -> p t", t=PACK))
-        nc.sync.dma_start(out=band_sb[:], in_=band.rearrange("(p t) -> p t", t=PACK))
-        with nc.allow_non_contiguous_dma(reason="one factor for each partition"):
-            nc.sync.dma_start(out=bub_sb[:], in_=bub.rearrange("(c p) -> p c", p=P))
-        load_tab(0)
         load_tab_scales()
-        load_wd(0)
+        load_tab(0)
         nc.sync.dma_start(
             out=w4_raw[:].bitcast(I32).rearrange("p (a n) -> p a n", a=PASSES),
             in_=w4_words.bitcast(I32).rearrange("a p n -> p a n"),
         )
-        load_scales(w4_sc_raw, w4_scales)
+        load_wd(0)
         load_wd(1)
         load_wd(2)
+        load_scales(w4_sc_raw, w4_scales)
         load_tab(1)
         load_tab(2)
+        nc.sync.dma_start(out=gain_sb[:], in_=gain.rearrange("(p t) -> p t", t=PACK))
+        nc.sync.dma_start(idx2[:], offs2)
         load_factors(0, 0, BANK)
         load_page(0)
         load_factors(0, BANK, S)
+        nc.sync.dma_start(idx4[:], offs4)
+        nc.sync.dma_start(idx3[:], offs3)
+        nc.sync.dma_start(out=band_sb[:], in_=band.rearrange("(p t) -> p t", t=PACK))
         for t in range(1, PACK):
             load_factors(t, 0, S)
             load_page(t)
+        with nc.allow_non_contiguous_dma(reason="one factor for each partition"):
+            nc.sync.dma_start(out=bub_sb[:], in_=bub.rearrange("(c p) -> p c", p=P))
 
         def gather_scales():
-            nc.vector.tensor_copy(v_sc[0][:], tab_sc[:].indirect(idx[:]))
-            for a in range(1, PASSES):
+            nc.vector.tensor_copy(v_rows[:], tab_sc[:].indirect(idx[:]))
+            for a in range(PASSES):
                 for q in range(P // QUAD):
-                    row = SPARE[a] + 4 * q
+                    row = FIRST_ROW + SCALE_ROWS * a + 4 * q
                     nc.gpsimd.dma_start(
-                        out=v_sc[a][QUAD * q : QUAD * q + 4, :].bitcast(I32),
-                        in_=v_sc[0][row : row + 4, :].bitcast(I32),
+                        out=v_sc[QUAD * q : QUAD * q + 4, a * S : (a + 1) * S].bitcast(I32),
+                        in_=v_rows[row : row + 4, :].bitcast(I32),
                     )
 
         def gather_words(a, lo, hi):
@@ -195,14 +192,14 @@ def tile_list_bubble_band_match_kernel(
                         out=acc[:],
                         lhsT=wd_q[a][:, t * P : (t + 1) * P].bitcast(FP8X4),
                         lhsT_scale=wd_sc[a][:, t * P : (t + 1) * P],
-                        rhs=moving, rhs_scale=v_sc[a][:, cols],
+                        rhs=moving, rhs_scale=v_sc[:, a * S + lo : a * S + lo + BANK],
                         start=(a == 0), stop=False,
                     )
                     nc.tensor.matmul_mx(
                         out=acc[:],
                         lhsT=w4[:, 2 * c0 : 2 * (c0 + P)].bitcast(FP4X4),
                         lhsT_scale=w4_sc[:, c0 : c0 + P],
-                        rhs=moving, rhs_scale=v_sc[a][:, cols],
+                        rhs=moving, rhs_scale=v_sc[:, a * S + lo : a * S + lo + BANK],
                         start=False, stop=(a == PASSES - 1),
                     )
                 nc.scalar.activation(out=bent[t][:, cols], in_=acc[:], func=ACT.Tanh)

@@ -22,6 +22,7 @@ PACK = 4
 PASSES = K // (P * PACK)
 BANK = 512
 QUAD = 32
+LEAD = 256
 SCALE_ROWS = 16
 FIRST_ROW = P - PASSES * SCALE_ROWS
 
@@ -35,8 +36,8 @@ def tile_list_bubble_band_match_kernel(
         keep = ctx.enter_context(tc.tile_pool(name="keep", bufs=1))
         psum = ctx.enter_context(tc.psum_pool(name="psum", bufs=1))
 
-        def tile(name, shape, dtype):
-            return keep.tile(shape, dtype, name=name, align_bytes=64)
+        def tile(name, shape, dtype, tag=""):
+            return keep.tile(shape, dtype, name=name, tag=tag or name, align_bytes=64)
 
         def tiles(name, count, shape, dtype):
             return [tile(f"{name}{i}", shape, dtype) for i in range(count)]
@@ -53,7 +54,6 @@ def tile_list_bubble_band_match_kernel(
         w4_raw = tile("w4_raw", [P, PASSES * 2 * H], U8)
         w4_sc_raw = tile("w4_sc_raw", [P, PASSES * H], U8)
         w4 = tile("w4", [P, PASSES * 2 * H], U8)
-        w4_sc = tile("w4_sc", [P, PASSES * H], U8)
         wd_raw = tiles("wd_raw", PASSES, [P, PACK, H], F32)
         wd_bf = tiles("wd_bf", PASSES, [P, PACK * H], BF16)
         wd_q = tiles("wd_q", PASSES, [P, H], U32)
@@ -82,7 +82,7 @@ def tile_list_bubble_band_match_kernel(
 
         def load_scales(dst, src):
             for q in range(P // QUAD):
-                nc.sync.dma_start(
+                nc.gpsimd.dma_start(
                     out=dst[QUAD * q : QUAD * q + 4, :].bitcast(I32).rearrange("r (a n) -> r a n", a=PASSES),
                     in_=src.bitcast(I32)[:, 4 * q : 4 * q + 4, :].rearrange("a r n -> r a n"),
                 )
@@ -119,16 +119,16 @@ def tile_list_bubble_band_match_kernel(
             in_=w4_words.bitcast(I32).rearrange("a p n -> p a n"),
         )
         load_wd(0)
-        load_wd(1)
-        load_wd(2)
         load_scales(w4_sc_raw, w4_scales)
+        load_wd(1)
         load_tab(1)
+        load_wd(2)
         load_tab(2)
         nc.sync.dma_start(out=gain_sb[:], in_=gain.rearrange("(p t) -> p t", t=PACK))
         nc.sync.dma_start(idx2[:], offs2)
-        load_factors(0, 0, BANK)
+        load_factors(0, 0, LEAD)
         load_page(0)
-        load_factors(0, BANK, S)
+        load_factors(0, LEAD, S)
         nc.sync.dma_start(idx4[:], offs4)
         nc.sync.dma_start(idx3[:], offs3)
         nc.sync.dma_start(out=band_sb[:], in_=band.rearrange("(p t) -> p t", t=PACK))
@@ -153,38 +153,46 @@ def tile_list_bubble_band_match_kernel(
                 v_words[a][:, lo:hi], tab[a][:].bitcast(U32).indirect(idx[:, lo // 16 : hi // 16])
             )
 
-        def round_wd(a):
+        def round_wd(a, t0, t1):
             nc.scalar.copy(
-                out=wd_bf[a][:].rearrange("p (t m j) -> p m t j", t=PACK, j=PACK),
-                in_=wd_raw[a][:].rearrange("p j (m t) -> p m t j", t=PACK),
+                out=wd_bf[a][:].rearrange("p (t m j) -> p m t j", t=PACK, j=PACK)[:, :, t0:t1, :],
+                in_=wd_raw[a][:].rearrange("p j (m t) -> p m t j", t=PACK)[:, :, t0:t1, :],
             )
 
-        def quantize_wd(a):
-            nc.vector.quantize_mx(out=wd_q[a][:].bitcast(FP8X4), scales=wd_sc[a][:], in_=wd_bf[a][:])
+        def quantize_wd(a, t0, t1):
+            cols = slice(t0 * P, t1 * P)
+            nc.vector.quantize_mx(
+                out=wd_q[a][:, cols].bitcast(FP8X4), scales=wd_sc[a][:, cols],
+                in_=wd_bf[a][:, t0 * P * PACK : t1 * P * PACK],
+            )
 
-        for a in range(PASSES):
-            round_wd(a)
+        round_wd(0, 0, PACK)
+        round_wd(1, 0, PACK)
+        round_wd(2, 0, PACK // 2)
+        round_wd(2, PACK // 2, PACK)
         gather_scales()
         gather_words(0, 0, S)
         nc.vector.tensor_copy(
             out=w4[:].bitcast(U16).rearrange("p (a t m) -> p a t m", a=PASSES, t=PACK),
             in_=w4_raw[:].bitcast(U16).rearrange("p (a m t) -> p a t m", a=PASSES, t=PACK),
         )
+        w4_sc = tile("w4_sc", [P, PASSES * H], U8, tag="tab0")
         nc.vector.tensor_copy(
             out=w4_sc[:].rearrange("p (a t m) -> p a t m", a=PASSES, t=PACK),
             in_=w4_sc_raw[:].rearrange("p (a m t) -> p a t m", a=PASSES, t=PACK),
         )
-        quantize_wd(0)
-        quantize_wd(1)
-        quantize_wd(2)
+        quantize_wd(0, 0, PACK)
+        quantize_wd(1, 0, PACK)
         gather_words(1, 0, S)
+        quantize_wd(2, 0, PACK // 2)
         gather_words(2, 0, BANK)
         gather_words(2, BANK, S)
+        quantize_wd(2, PACK // 2, PACK)
 
         for t in range(PACK):
             for lo in range(0, S, BANK):
                 cols = slice(lo, lo + BANK)
-                acc = psum.tile([P, BANK], F32, name="acc", bufs=2)
+                acc = psum.tile([P, BANK], F32, name="acc", bufs=4)
                 for a in range(PASSES):
                     c0 = a * H + t * P
                     moving = v_words[a][:, cols].bitcast(FP8X4)
@@ -227,11 +235,11 @@ def tile_list_bubble_band_match_kernel(
                 page[t][:].indirect(idx2[:, lo // 16 : hi // 16]), h[:, lo:hi], wgs_sb[t][:, lo:hi], MULT
             )
 
-        finish_h(0, 0, BANK)
-        put(0, 0, BANK)
-        finish_h(0, BANK, S)
+        finish_h(0, 0, LEAD)
+        put(0, 0, LEAD)
+        finish_h(0, LEAD, S)
         for t in range(PACK):
-            put(t, BANK if t == 0 else 0, S)
+            put(t, LEAD if t == 0 else 0, S)
             if t + 1 < PACK:
                 nc.gpsimd.tensor_tensor(h[:], bent[t + 1][:], res_sb[t + 1][:], ADD)
                 pick_bands(t, 0, PICKS)

from contextlib import ExitStack

import concourse.mybir as mybir

K, H, T, S, T2, PICKS = 1536, 512, 2048, 1024, 2048, 512
FLOPS = 2 * (2 * K * H * S) + 2 * H * PICKS * PICKS

F32 = mybir.dt.float32
BF16 = mybir.dt.bfloat16
I32 = mybir.dt.int32
U32 = mybir.dt.uint32
U16 = mybir.dt.uint16
U8 = mybir.dt.uint8
FP8X4 = mybir.dt.float8_e4m3fn_x4
FP4X4 = mybir.dt.float4_e2m1fn_x4
MULT = mybir.AluOpType.mult
ADD = mybir.AluOpType.add
ACT = mybir.ActivationFunctionType

P = 128
PACK = 4
PASSES = K // (P * PACK)
BANK = 512
QUAD = 32
LEAD = 256
SCALE_ROWS = 16
FIRST_ROW = P - PASSES * SCALE_ROWS


def tile_list_bubble_band_match_kernel(
    tc, tab_words, tab_scales, w4_words, w4_scales, wd, gain, res, page0, wgs, band, bub,
    offs, offs2, offs3, offs4, out,
):
    nc = tc.nc
    with ExitStack() as ctx:
        keep = ctx.enter_context(tc.tile_pool(name="keep", bufs=1))
        psum = ctx.enter_context(tc.psum_pool(name="psum", bufs=1))

        def tile(name, shape, dtype, tag=""):
            return keep.tile(shape, dtype, name=name, tag=tag or name, align_bytes=64)

        def tiles(name, count, shape, dtype):
            return [tile(f"{name}{i}", shape, dtype) for i in range(count)]

        idx = tile("idx", [P, S // 16], U16)
        idx2 = tile("idx2", [P, S // 16], U16)
        idx3 = tile("idx3", [P, PICKS // 16], U16)
        idx4 = tile("idx4", [P, PICKS // 16], U16)
        tab = tiles("tab", PASSES, [P, T], I32)
        tab_sc = tile("tab_sc", [P, T], U8)
        v_words = tiles("v_words", PASSES, [P, S], U32)
        v_rows = tile("v_rows", [P, S], U8)
        v_sc = tile("v_sc", [P, PASSES * S], U8)
        w4_raw = tile("w4_raw", [P, PASSES * 2 * H], U8)
        w4_sc_raw = tile("w4_sc_raw", [P, PASSES * H], U8)
        w4 = tile("w4", [P, PASSES * 2 * H], U8)
        wd_raw = tiles("wd_raw", PASSES, [P, PACK, H], F32)
        wd_bf = tiles("wd_bf", PASSES, [P, PACK * H], BF16)
        wd_q = tiles("wd_q", PASSES, [P, H], U32)
        wd_sc = tiles("wd_sc", PASSES, [P, H], U8)
        gain_sb = tile("gain_sb", [P, PACK], F32)
        band_sb = tile("band_sb", [P, PACK], F32)
        bub_sb = tile("bub_sb", [P, PICKS // P], F32)
        page = tiles("page", PACK, [P, T2], F32)
        res_sb = tiles("res_sb", PACK, [P, S], F32)
        wgs_sb = tiles("wgs_sb", PACK, [P, S], F32)
        bent = tiles("bent", PACK, [P, S], F32)
        h = tile("h", [P, S], F32)
        picked = tiles("picked", 2, [P, PICKS], F32)
        size = tile("size", [P, PICKS], F32)
        x1_bf = tile("x1_bf", [P, PICKS, PACK], BF16)
        x2_bf = tile("x2_bf", [P, PICKS, PACK], BF16)
        x1_q = tile("x1_q", [P, PICKS], U32)
        x2_q = tile("x2_q", [P, PICKS], U32)
        x1_sc = tile("x1_sc", [P, PICKS], U8)
        x2_sc = tile("x2_sc", [P, PICKS], U8)
        out_sb = tiles("out_sb", PICKS // P, [P, PICKS], F32)

        nc.vector.memset(w4_sc_raw[:].bitcast(I32), 0)
        nc.vector.memset(tab_sc[0:FIRST_ROW, :].bitcast(I32), 0)
        nc.vector.memset(v_sc[:].bitcast(I32), 0)

        def load_scales(dst, src):
            for q in range(P // QUAD):
                nc.gpsimd.dma_start(
                    out=dst[QUAD * q : QUAD * q + 4, :].bitcast(I32).rearrange("r (a n) -> r a n", a=PASSES),
                    in_=src.bitcast(I32)[:, 4 * q : 4 * q + 4, :].rearrange("a r n -> r a n"),
                )

        def load_wd(a):
            rows = wd[a * P * PACK : (a + 1) * P * PACK, :]
            nc.sync.dma_start(out=wd_raw[a][:], in_=rows.rearrange("(p j) c -> p j c", j=PACK))

        def load_tab(a):
            nc.sync.dma_start(out=tab[a][:], in_=tab_words[a].rearrange("p n i -> p (n i)").bitcast(I32))

        res_rows = res.rearrange("(p t) n -> t p n", t=PACK)
        page_rows = page0.rearrange("(p t) n -> t p n", t=PACK)
        wgs_rows = wgs.rearrange("(e t) n -> t e n", t=PACK)

        def load_factors(t, lo, hi):
            nc.sync.dma_start(out=res_sb[t][:, lo:hi], in_=res_rows[t][:, lo:hi])
            for q in range(P // QUAD):
                nc.sync.dma_start(out=wgs_sb[t][QUAD * q : QUAD * (q + 1), lo:hi], in_=wgs_rows[t][:, lo:hi])

        def load_page(t):
            nc.sync.dma_start(out=page[t][:], in_=page_rows[t])

        def load_tab_scales():
            rows = tab_scales.bitcast(I32).rearrange("a q n -> (a q) n")
            for lo, hi in ((0, SCALE_ROWS), (SCALE_ROWS, PASSES * SCALE_ROWS)):
                nc.sync.dma_start(out=tab_sc[FIRST_ROW + lo : FIRST_ROW + hi, :].bitcast(I32), in_=rows[lo:hi, :])

        nc.sync.dma_start(idx[:], offs)
        load_tab_scales()
        load_tab(0)
        nc.sync.dma_start(
            out=w4_raw[:].bitcast(I32).rearrange("p (a n) -> p a n", a=PASSES),
            in_=w4_words.bitcast(I32).rearrange("a p n -> p a n"),
        )
        load_wd(0)
        load_scales(w4_sc_raw, w4_scales)
        load_wd(1)
        load_tab(1)
        load_wd(2)
        load_tab(2)
        nc.sync.dma_start(out=gain_sb[:], in_=gain.rearrange("(p t) -> p t", t=PACK))
        nc.sync.dma_start(idx2[:], offs2)
        load_factors(0, 0, LEAD)
        load_page(0)
        load_factors(0, LEAD, S)
        nc.sync.dma_start(idx4[:], offs4)
        nc.sync.dma_start(idx3[:], offs3)
        nc.sync.dma_start(out=band_sb[:], in_=band.rearrange("(p t) -> p t", t=PACK))
        for t in range(1, PACK):
            load_factors(t, 0, S)
            load_page(t)
        with nc.allow_non_contiguous_dma(reason="one factor for each partition"):
            nc.sync.dma_start(out=bub_sb[:], in_=bub.rearrange("(c p) -> p c", p=P))

        def gather_scales():
            nc.vector.tensor_copy(v_rows[:], tab_sc[:].indirect(idx[:]))
            for a in range(PASSES):
                for q in range(P // QUAD):
                    row = FIRST_ROW + SCALE_ROWS * a + 4 * q
                    nc.gpsimd.dma_start(
                        out=v_sc[QUAD * q : QUAD * q + 4, a * S : (a + 1) * S].bitcast(I32),
                        in_=v_rows[row : row + 4, :].bitcast(I32),
                    )

        def gather_words(a, lo, hi):
            nc.vector.tensor_copy(
                v_words[a][:, lo:hi], tab[a][:].bitcast(U32).indirect(idx[:, lo // 16 : hi // 16])
            )

        def round_wd(a, t0, t1):
            nc.scalar.copy(
                out=wd_bf[a][:].rearrange("p (t m j) -> p m t j", t=PACK, j=PACK)[:, :, t0:t1, :],
                in_=wd_raw[a][:].rearrange("p j (m t) -> p m t j", t=PACK)[:, :, t0:t1, :],
            )

        def quantize_wd(a, t0, t1):
            cols = slice(t0 * P, t1 * P)
            nc.vector.quantize_mx(
                out=wd_q[a][:, cols].bitcast(FP8X4), scales=wd_sc[a][:, cols],
                in_=wd_bf[a][:, t0 * P * PACK : t1 * P * PACK],
            )

        round_wd(0, 0, PACK)
        round_wd(1, 0, PACK)
        round_wd(2, 0, PACK // 2)
        round_wd(2, PACK // 2, PACK)
        gather_scales()
        gather_words(0, 0, S)
        nc.vector.tensor_copy(
            out=w4[:].bitcast(U16).rearrange("p (a t m) -> p a t m", a=PASSES, t=PACK),
            in_=w4_raw[:].bitcast(U16).rearrange("p (a m t) -> p a t m", a=PASSES, t=PACK),
        )
        w4_sc = tile("w4_sc", [P, PASSES * H], U8, tag="tab0")
        nc.vector.tensor_copy(
            out=w4_sc[:].rearrange("p (a t m) -> p a t m", a=PASSES, t=PACK),
            in_=w4_sc_raw[:].rearrange("p (a m t) -> p a t m", a=PASSES, t=PACK),
        )
        quantize_wd(0, 0, PACK)
        quantize_wd(1, 0, PACK)
        gather_words(1, 0, S)
        quantize_wd(2, 0, PACK // 2)
        gather_words(2, 0, BANK)
        gather_words(2, BANK, S)
        quantize_wd(2, PACK // 2, PACK)

        for t in range(PACK):
            for lo in range(0, S, BANK):
                cols = slice(lo, lo + BANK)
                acc = psum.tile([P, BANK], F32, name="acc", bufs=4)
                for a in range(PASSES):
                    c0 = a * H + t * P
                    moving = v_words[a][:, cols].bitcast(FP8X4)
                    nc.tensor.matmul_mx(
                        out=acc[:],
                        lhsT=wd_q[a][:, t * P : (t + 1) * P].bitcast(FP8X4),
                        lhsT_scale=wd_sc[a][:, t * P : (t + 1) * P],
                        rhs=moving, rhs_scale=v_sc[:, a * S + lo : a * S + lo + BANK],
                        start=(a == 0), stop=False,
                    )
                    nc.tensor.matmul_mx(
                        out=acc[:],
                        lhsT=w4[:, 2 * c0 : 2 * (c0 + P)].bitcast(FP4X4),
                        lhsT_scale=w4_sc[:, c0 : c0 + P],
                        rhs=moving, rhs_scale=v_sc[:, a * S + lo : a * S + lo + BANK],
                        start=False, stop=(a == PASSES - 1),
                    )
                nc.scalar.activation(out=bent[t][:, cols], in_=acc[:], func=ACT.Tanh)
                if t > 0:
                    nc.scalar.activation(
                        out=bent[t][:, cols], in_=bent[t][:, cols], func=ACT.Copy, scale=gain_sb[:, t : t + 1]
                    )

        def finish_h(t, lo, hi):
            nc.vector.scalar_tensor_tensor(
                out=h[:, lo:hi], in0=bent[t][:, lo:hi], scalar=gain_sb[:, t : t + 1],
                in1=res_sb[t][:, lo:hi], op0=MULT, op1=ADD,
            )

        def pick_bands(t, lo, hi):
            dst = picked[t % 2]
            nc.vector.tensor_copy(dst[:, lo:hi], page[t][:].indirect(idx4[:, lo // 16 : hi // 16]))
            nc.scalar.activation(out=size[:, lo:hi], in_=dst[:, lo:hi], func=ACT.Abs)
            nc.scalar.activation(
                out=x2_bf[:, lo:hi, t], in_=size[:, lo:hi], func=ACT.Copy, scale=band_sb[:, t : t + 1]
            )

        def put(t, lo, hi):
            nc.vector.tensor_tensor(
                page[t][:].indirect(idx2[:, lo // 16 : hi // 16]), h[:, lo:hi], wgs_sb[t][:, lo:hi], MULT
            )

        finish_h(0, 0, LEAD)
        put(0, 0, LEAD)
        finish_h(0, LEAD, S)
        for t in range(PACK):
            put(t, LEAD if t == 0 else 0, S)
            if t + 1 < PACK:
                nc.gpsimd.tensor_tensor(h[:], bent[t + 1][:], res_sb[t + 1][:], ADD)
                pick_bands(t, 0, PICKS)
                dst = picked[(t + 1) % 2]
                nc.vector.tensor_copy(dst[:], page[t][:].indirect(idx3[:]))
                nc.scalar.copy(out=x1_bf[:, :, t], in_=dst[:])
            else:
                pick_bands(t, 0, PICKS // 2)
                pick_bands(t, PICKS // 2, PICKS)
                nc.vector.tensor_copy(x1_bf[:, :, t], page[t][:].indirect(idx3[:]))

        def quantize(codes, scales, values, lo, hi):
            nc.vector.quantize_mx(
                out=codes[:, lo:hi].bitcast(FP8X4), scales=scales[:, lo:hi],
                in_=values[:, lo:hi, :].rearrange("p n t -> p (n t)"),
            )

        half = PICKS // 2
        quantize(x2_q, x2_sc, x2_bf, 0, half)
        quantize(x1_q, x1_sc, x1_bf, 0, PICKS)
        quantize(x2_q, x2_sc, x2_bf, half, PICKS)

        for c in range(PICKS // P):
            rows = slice(c * P, (c + 1) * P)
            acc = psum.tile([P, BANK], F32, name="score", bufs=4)
            nc.tensor.matmul_mx(
                out=acc[:], lhsT=x1_q[:, rows].bitcast(FP8X4), lhsT_scale=x1_sc[:, rows],
                rhs=x2_q[:].bitcast(FP8X4), rhs_scale=x2_sc[:], start=True, stop=True,
            )
            if c % 2 == 0:
                nc.scalar.activation(out=out_sb[c][:], in_=acc[:], func=ACT.Copy, scale=bub_sb[:, c : c + 1])
            else:
                nc.vector.tensor_scalar(
                    out=out_sb[c][:], in0=acc[:], scalar1=bub_sb[:, c : c + 1], scalar2=None, op0=MULT
                )
            nc.sync.dma_start(out=out[rows, :], in_=out_sb[c][:])
